import numpy as np
import ml_dtypes


def mxq(x, axis, fmt="e4m3"):
    dtype, down = {"e4m3": (ml_dtypes.float8_e4m3fn, 7), "e5m2": (ml_dtypes.float8_e5m2, 14)}[fmt]
    v = np.moveaxis(np.asarray(x, np.float32).astype(ml_dtypes.bfloat16).astype(np.float64), axis, -1)
    blocks = v.reshape(v.shape[:-1] + (-1, 32))
    amax = np.abs(blocks).max(-1, keepdims=True)
    byte = np.maximum(np.where(amax > 0, np.frexp(amax)[1] - 1 + 127, 0) - down, 1)
    scale = np.exp2(byte - 127.0)
    codes = (blocks / scale).astype(np.float32).astype(dtype).astype(np.float64)
    return np.moveaxis((codes * scale).reshape(v.shape), -1, axis)


WIDE = False


def mx_kscale(k):
    if not WIDE:
        return np.ones(k)
    levels = np.array([10, -10, 5, -5, 0])
    if k % 512:
        return np.exp2(np.random.permutation(np.resize(levels, k // 32))).repeat(32)
    a = np.empty((k // 512, 16))
    for p in range(k // 512):
        a[p, :8] = np.random.permutation(np.resize(levels, 8))
        for g in range(8):
            far = levels[np.abs(levels - a[p, g]) >= 10]
            a[p, g + 8] = far[np.random.randint(len(far))]
    return np.exp2(a.ravel()).repeat(32)


def f64(x):
    return np.asarray(x).astype(np.float64)


def striped(idx):
    return np.tile(idx.reshape(-1, 16).T, (8, 1)).astype(np.uint16)


def unstriped(offs):
    return offs[:16].T.reshape(-1).astype(np.int64)


def striped8(idx):
    return np.concatenate([x.reshape(-1, 16).T for x in idx]).astype(np.uint16)


def runs(offs, k):
    lists = np.stack([offs[16 * r : 16 * r + 16].T.reshape(-1) for r in range(8)]).astype(np.int64)
    return lists[np.arange(k) % 512 // 64]


def pack_weight(w):
    k, n = w.shape
    w = f64(np.asarray(w, np.float32).astype(ml_dtypes.bfloat16)).reshape(k // 32, 32, n)
    amax = np.abs(w).max(1)
    byte = np.clip(np.where(amax > 0, np.frexp(amax)[1] - 1 + 127 - 7, 1), 1, 254)
    scaled = (w * np.exp2(127.0 - byte)[:, None, :]).reshape(k, n).astype(np.float32)
    words = np.ascontiguousarray(scaled.reshape(k // 512, 128, 4, n).transpose(0, 1, 3, 2)).astype(ml_dtypes.float8_e4m3fn).view(np.uint8)
    return words, np.ascontiguousarray(byte.astype(np.uint8).reshape(k // 512, 16, n))


def unpack_weight(words, scales):
    g, p, n, _ = words.shape
    vals = np.ascontiguousarray(words).view(ml_dtypes.float8_e4m3fn).astype(np.float64) * np.repeat(np.exp2(scales.astype(np.float64) - 127.0), 8, axis=1)[..., None]
    return vals.transpose(0, 1, 3, 2).reshape(g * 512, n)

def planes(y):
    n, m = y.shape
    v = y.astype(np.float32).astype(ml_dtypes.bfloat16).astype(np.float64).reshape(n // 32, 32, m)
    top = np.abs(v).max(1)
    byte = np.clip(np.where(top > 0, np.frexp(top)[1] - 1 + 127 - 7, 1), 1, 254)
    codes = (v * np.exp2(127.0 - byte)[:, None, :]).reshape(n, m).astype(np.float32).astype(ml_dtypes.float8_e4m3fn).view(np.uint8)
    words = codes.reshape(n // 512, 128, 4, m).transpose(0, 1, 3, 2)
    return np.ascontiguousarray(words), np.ascontiguousarray(byte.astype(np.uint8).reshape(n // 512, 16, m))


K, T, S, N, H, W, U = 512, 2048, 512, 512, 512, 256, 1024


def setup_inputs():
    n = np.random.standard_normal
    s = mx_kscale(K)[:, None]
    u = mx_kscale(S)
    packed_xT = pack_weight(n((K, T)) * s)
    perm = np.stack([np.random.permutation(H) for _ in range(8)])
    return {
        "x_words": packed_xT[0],
        "x_scales": packed_xT[1],
        "wa": (n((K, H)) / np.sqrt(K) / s).astype(np.float32),
        "wb": (n((K, N)) / np.sqrt(K) / s).astype(np.float32),
        "gt": (np.random.uniform(0.5, 1.5, (S, 1)) * u[:, None]).astype(np.float32),
        "gi": (np.random.uniform(0.5, 1.5, (S, 1)) / u[:, None]).astype(np.float32),
        "mem": n((H, U)).astype(np.float32),
        "offs": striped(np.random.permutation(T)[:S]),
        "two": striped(np.random.permutation(T)[:S]),
        "n1": striped8(perm[:, :W]),
        "n2": striped8(perm[:, W:]),
        "n3": striped8(np.stack([np.random.permutation(U)[:N] for _ in range(8)])),
    }


def reference(x_words, x_scales, wa, wb, gt, gi, mem, offs, two, n1, n2, n3):
    xq = unpack_weight(x_words, x_scales)[:, unstriped(offs)]
    a = xq.T @ mxq(f64(wa), 0, "e4m3")
    pa = a[np.arange(S)[:, None], runs(n1, S)]
    pb = a[np.arange(S)[:, None], runs(n2, S)]
    rb = pa * pb
    ra = pa + pb
    ds = np.zeros((S, H))
    ds[np.arange(S)[:, None], runs(n1, S)] = ra
    dt = ds.copy()
    dt[np.arange(S)[:, None], runs(n2, S)] = rb
    z = f64(gt) * dt
    x_two = unpack_weight(x_words, x_scales)[:, unstriped(two)]
    b = x_two.T @ mxq(f64(wb), 0, "e4m3")
    z2 = f64(gi) * b
    cv = 0.0625 * ((mxq(z, 0, "e4m3").T @ mxq(z2, 0, "e4m3")))
    nw = np.maximum(cv, 0.5 * (f64(mem)[np.arange(H)[:, None], runs(n3, H)]))
    out = f64(mem).copy()
    out[np.arange(H)[:, None], runs(n3, H)] = nw
    return (out,) + planes(out)

@@ -1,0 +1,218 @@
+from contextlib import ExitStack
+
+import concourse.mybir as mybir
+
+K, T, S, N, H, W, U = 512, 2048, 512, 512, 512, 256, 1024
+FLOPS = 2 * K * S * H + 2 * K * S * N + 2 * S * H * N
+
+F32 = mybir.dt.float32
+BF16 = mybir.dt.bfloat16
+I32 = mybir.dt.int32
+U32 = mybir.dt.uint32
+U16 = mybir.dt.uint16
+U8 = mybir.dt.uint8
+FP8X4 = mybir.dt.float8_e4m3fn_x4
+ALU = mybir.AluOpType
+COPY = mybir.ActivationFunctionType.Copy
+
+P = 128
+PACK = 4
+HALF = 256
+CHUNK = 256
+CHUNKS = U // CHUNK
+VECTOR_CHUNKS = 2
+
+
+def tile_picked_mombondpagex_none_po_kernel(tc, x_words, x_scales, wa, wb, gt, gi, mem, offs, two, n1, n2, n3, out_0, out_1, out_2):
+    nc = tc.nc
+    with ExitStack() as ctx:
+        keep = ctx.enter_context(tc.tile_pool(name="keep", bufs=1))
+        shared = ctx.enter_context(tc.tile_pool(name="shared", bufs=1))
+        psum = ctx.enter_context(tc.psum_pool(name="psum", bufs=4))
+
+        def sb(name, shape, dtype, tag=None):
+            return keep.tile(shape, dtype, name=name, tag=tag or name, align_bytes=64)
+
+        def placed(name, shape, dtype, offset):
+            return shared.tile(shape, dtype, name=name, align_bytes=64, offset=offset)
+
+        def load_list(name, src):
+            tile = sb(name, list(src.shape), U16)
+            nc.sync.dma_start(tile[:], src)
+            return tile
+
+        mem_rows = mem.rearrange("(p t) u -> t p u", t=PACK)
+        out_rows = out_0.rearrange("(p t) u -> t p u", t=PACK)
+        page = [sb(f"page{t}", [P, U], F32) for t in range(PACK)]
+
+        def load_page(t):
+            nc.sync.dma_start(page[t][:], mem_rows[t])
+
+        def load_weight_half(name, w, h):
+            raw = sb(f"{name}_raw{h}", [P, PACK, HALF], F32)
+            nc.sync.dma_start(raw[:], w.rearrange("(p j) c -> p j c", j=PACK)[:, :, h * HALF:(h + 1) * HALF])
+            return raw
+
+        x_bytes = sb("x_bytes", [P, T], U8)
+        nc.vector.memset(x_bytes[:].bitcast(I32), 0)
+        n3_t = load_list("n3_t", n3)
+        load_page(0)
+        offs_t = load_list("offs_t", offs)
+        x_codes = sb("x_codes", [P, T], I32)
+        nc.sync.dma_start(x_codes[:], x_words[0].rearrange("p c r -> p (c r)").bitcast(I32))
+        for q in range(4):
+            nc.scalar.dma_start(x_bytes[32 * q:32 * q + 4, :].bitcast(I32), x_scales[0, 4 * q:4 * q + 4, :].bitcast(I32))
+        two_t = load_list("two_t", two)
+        wa_raw = [load_weight_half("wa", wa, h) for h in range(2)]
+        load_page(1)
+        n1_t = load_list("n1_t", n1)
+        n2_t = load_list("n2_t", n2)
+        wb_raw = [load_weight_half("wb", wb, h) for h in range(2)]
+        gt_t = sb("gt_t", [P, PACK], F32)
+        nc.sync.dma_start(gt_t[:], gt.rearrange("(p t) o -> p (t o)", t=PACK))
+        gi_t = sb("gi_t", [P, PACK], F32)
+        nc.sync.dma_start(gi_t[:], gi.rearrange("(p t) o -> p (t o)", t=PACK))
+        load_page(2)
+        load_page(3)
+
+        held = [None] * PACK
+
+        def fetch_held(t, tile):
+            held[t] = tile
+            nc.vector.tensor_scalar(held[t][:], page[t][:].indirect(n3_t[:]), 0.5, 0.0, ALU.mult, ALU.add)
+
+        def pick_tokens(name, offsets):
+            listed = sb(f"{name}_listed", [P, S], U8)
+            nc.vector.tensor_copy(listed[:], x_bytes[:].indirect(offsets[:]))
+            codes = sb(f"{name}_codes", [P, S], U32)
+            nc.vector.tensor_copy(codes[:].rearrange("p (t m) -> p m t", t=PACK), x_codes[:].bitcast(U32).indirect(offsets[:]))
+            scales = sb(f"{name}_scales", [P, S], U8)
+            nc.vector.tensor_copy(scales[:].rearrange("p (t m) -> p t m", t=PACK), listed[:].rearrange("p (m t) -> p t m", t=PACK))
+            return codes, scales
+
+        def quantize(codes, scales, grouped):
+            nc.vector.quantize_mx(out=codes.bitcast(FP8X4), scales=scales, in_=grouped.rearrange("p c t -> p (c t)"))
+
+        def interleave(grouped, planes):
+            nc.scalar.copy(grouped.rearrange("p (c i) t -> p c t i", i=4), planes.rearrange("p t (c i) -> p c t i", i=4))
+
+        def quantize_weight(name, raw):
+            codes = sb(f"{name}_codes", [P, 2 * HALF], U32)
+            scales = sb(f"{name}_scales", [P, 2 * HALF], U8)
+            for h in range(2):
+                grouped = sb(f"{name}_grouped{h}", [P, HALF, PACK], BF16)
+                interleave(grouped[:], raw[h][:])
+                cols = slice(h * HALF, (h + 1) * HALF)
+                quantize(codes[:, cols], scales[:, cols], grouped[:])
+            return codes, scales
+
+        def product(tag, left, right, t):
+            acc = psum.tile([P, 512], F32, name=f"{tag}_acc", tag=tag)
+            cols = slice(t * P, (t + 1) * P)
+            nc.tensor.matmul_mx(out=acc[:], lhsT=left[0][:, cols].bitcast(FP8X4), lhsT_scale=left[1][:, cols],
+                                rhs=right[0][:].bitcast(FP8X4), rhs_scale=right[1][:], start=True, stop=True)
+            return acc
+
+        fetch_held(0, sb("held0", [P, N], F32))
+        xa = pick_tokens("xa", offs_t)
+        xb = pick_tokens("xb", two_t)
+        wa_q = quantize_weight("wa", wa_raw)
+        a = []
+        for t in range(PACK):
+            acc = product("first", xa, wa_q, t)
+            a.append(sb(f"a{t}", [P, H], F32))
+            nc.scalar.copy(a[t][:], acc[:])
+        fetch_held(1, sb("held1", [P, N], F32, "wa_grouped1"))
+
+        pa = [sb("pa0", [P, W], F32)]
+        pb = [sb(f"pb{t}", [P, W], F32) for t in range(PACK)]
+        dt = [sb(f"dt{t}", [P, H], F32) for t in range(PACK)]
+
+        def fetch(dst, t, offsets):
+            nc.vector.tensor_copy(dst[t][:], a[t][:].indirect(offsets[:]))
+
+        def put(t, offsets, op):
+            nc.vector.tensor_tensor(dt[t][:].indirect(offsets[:]), pa[t][:], pb[t][:], op)
+
+        def round_z(t):
+            nc.scalar.activation(
+                z_grouped[:, :, t].rearrange("p (r m i) -> p m r i", r=PACK, i=2),
+                dt[t][:].rearrange("p (m i r) -> p m r i", r=PACK, i=2),
+                COPY, scale=gt_t[:, t:t + 1])
+
+        fetch(pa, 0, n1_t)
+        fetch(pb, 0, n2_t)
+        fetch(pb, 1, n2_t)
+        put(0, n1_t, ALU.add)
+        fetch(pb, 2, n2_t)
+        put(0, n2_t, ALU.mult)
+        fetch(pb, 3, n2_t)
+        wb_grouped = placed("wb_grouped", [P, N, PACK], BF16, 0)
+        for h in range(2):
+            interleave(wb_grouped[:, h * HALF:(h + 1) * HALF, :], wb_raw[h][:])
+        wb_q = (sb("wb_codes", [P, N], U32), sb("wb_scales", [P, N], U8))
+        quantize(wb_q[0][:], wb_q[1][:], wb_grouped[:])
+        pa.extend(placed(f"pa{t}", [P, W], F32, 4 * W * t) for t in range(1, PACK))
+        z2_planes = sb("z2_planes", [P, PACK, N], BF16)
+        for t in range(PACK):
+            acc = product("second", xb, wb_q, t)
+            nc.scalar.activation(z2_planes[:, t, :], acc[:], COPY, scale=gi_t[:, t:t + 1])
+        z2_grouped = sb("z2_grouped", [P, N, PACK], BF16)
+        interleave(z2_grouped[:], z2_planes[:])
+        z_grouped = sb("z_grouped", [P, H, PACK], BF16, "z2_planes")
+        round_z(0)
+        fetch(pa, 1, n1_t)
+        fetch(pa, 2, n1_t)
+        put(1, n1_t, ALU.add)
+        fetch(pa, 3, n1_t)
+        put(1, n2_t, ALU.mult)
+        round_z(1)
+        put(2, n1_t, ALU.add)
+        put(3, n1_t, ALU.add)
+        put(2, n2_t, ALU.mult)
+        round_z(2)
+        z2_q = (sb("z2_codes", [P, N], U32), sb("z2_scales", [P, N], U8))
+        quantize(z2_q[0][:], z2_q[1][:], z2_grouped[:])
+        put(PACK - 1, n2_t, ALU.mult)
+        round_z(PACK - 1)
+        fetch_held(2, placed("held2", [P, N], F32, 4 * W * (PACK - 1)))
+        z_q = (sb("z_codes", [P, H], U32), sb("z_scales", [P, H], U8))
+        quantize(z_q[0][:], z_q[1][:], z_grouped[:])
+        fetch_held(3, sb("held3", [P, N], F32, "z2_planes"))
+
+        out_grouped = [sb(f"out_grouped{c}", [P, CHUNK, PACK], BF16) for c in range(CHUNKS)]
+        nw = [sb(f"nw{t}", [P, N], F32) for t in range(PACK)]
+
+        def larger(t):
+            acc = product("first", z_q, z2_q, t)
+            nc.vector.scalar_tensor_tensor(nw[t][:], acc[:], 0.0625, held[t][:], ALU.mult, ALU.max)
+
+        def write(t):
+            nc.vector.tensor_copy(page[t][:].indirect(n3_t[:]), nw[t][:])
+            nc.sync.dma_start(out_rows[t], page[t][:])
+            for c in range(CHUNKS):
+                src = page[t][:, c * CHUNK:(c + 1) * CHUNK]
+                if t == PACK - 1 and c < VECTOR_CHUNKS:
+                    nc.vector.tensor_copy(out_grouped[c][:, :, t], src)
+                elif t == PACK - 2 and c < VECTOR_CHUNKS:
+                    nc.scalar.copy(out_grouped[c][:, :, t:], src.unsqueeze(2).to_broadcast([P, CHUNK, 2]))
+                else:
+                    nc.scalar.copy(out_grouped[c][:, :, t], src)
+
+        larger(0)
+        for t in range(PACK):
+            if t + 1 < PACK:
+                larger(t + 1)
+            write(t)
+
+        out_scales = sb("out_scales", [P, U], U8)
+        words = out_1[0].rearrange("p c r -> p (c r)").bitcast(I32)
+        for h in range(2):
+            out_codes = sb(f"out_codes{h}", [P, 2 * CHUNK], I32)
+            for i in range(2):
+                c = 2 * h + i
+                quantize(out_codes[:, i * CHUNK:(i + 1) * CHUNK], out_scales[:, c * CHUNK:(c + 1) * CHUNK], out_grouped[c][:])
+            nc.sync.dma_start(words[:, 2 * h * CHUNK:2 * (h + 1) * CHUNK], out_codes[:])
+        for q in range(4):
+            queue = nc.sync if q % 2 else nc.scalar
+            queue.dma_start(out_2[0, 4 * q:4 * q + 4, :].bitcast(I32), out_scales[32 * q:32 * q + 4, :].bitcast(I32))

@@ -1,6 +1,7 @@
 from contextlib import ExitStack
 
 import concourse.mybir as mybir
+from concourse.masks import make_identity
 
 K, T, S, N, H, W, U = 512, 2048, 512, 512, 512, 256, 1024
 FLOPS = 2 * K * S * H + 2 * K * S * N + 2 * S * H * N
@@ -17,6 +18,7 @@ COPY = mybir.ActivationFunctionType.Copy
 
 P = 128
 PACK = 4
+RUN = 8
 HALF = 256
 CHUNK = 256
 CHUNKS = U // CHUNK
@@ -55,25 +57,32 @@ def tile_picked_mombondpagex_none_po_kernel(tc, x_words, x_scales, wa, wb, gt, g
 
         x_bytes = sb("x_bytes", [P, T], U8)
         nc.vector.memset(x_bytes[:].bitcast(I32), 0)
+        offs_t = load_list("offs_t", offs)
         n3_t = load_list("n3_t", n3)
         load_page(0)
-        offs_t = load_list("offs_t", offs)
+        for q in range(4):
+            nc.sync.dma_start(x_bytes[32 * q:32 * q + 4, :].bitcast(I32), x_scales[0, 4 * q:4 * q + 4, :].bitcast(I32))
+        two_t = load_list("two_t", two)
+        n1_t = load_list("n1_t", n1)
         x_codes = sb("x_codes", [P, T], I32)
         nc.sync.dma_start(x_codes[:], x_words[0].rearrange("p c r -> p (c r)").bitcast(I32))
-        for q in range(4):
-            nc.scalar.dma_start(x_bytes[32 * q:32 * q + 4, :].bitcast(I32), x_scales[0, 4 * q:4 * q + 4, :].bitcast(I32))
-        two_t = load_list("two_t", two)
         wa_raw = [load_weight_half("wa", wa, h) for h in range(2)]
         load_page(1)
-        n1_t = load_list("n1_t", n1)
         n2_t = load_list("n2_t", n2)
         wb_raw = [load_weight_half("wb", wb, h) for h in range(2)]
-        gt_t = sb("gt_t", [P, PACK], F32)
-        nc.sync.dma_start(gt_t[:], gt.rearrange("(p t) o -> p (t o)", t=PACK))
-        gi_t = sb("gi_t", [P, PACK], F32)
-        nc.sync.dma_start(gi_t[:], gi.rearrange("(p t) o -> p (t o)", t=PACK))
+        gate_rows = sb("gate_rows", [P, P], F32)
+        nc.gpsimd.memset(gate_rows[:], 0.0)
+        for i, gate in enumerate((gt, gi)):
+            nc.sync.dma_start(gate_rows[PACK * i:PACK * (i + 1), :].rearrange("t (q r) -> t q r", r=RUN),
+                                gate.rearrange("(q t r) o -> t q (r o)", t=PACK, r=RUN))
         load_page(2)
         load_page(3)
+        identity = sb("identity", [P, P], F32)
+        make_identity(nc, identity[:])
+        gate_acc = psum.tile([P, P], F32, name="gate_acc", tag="second")
+        nc.tensor.transpose(gate_acc[:], gate_rows[:], identity[:])
+        gates = sb("gates", [P, 2 * PACK], F32)
+        nc.scalar.copy(gates[:], gate_acc[:, :2 * PACK])
 
         held = [None] * PACK
 
@@ -81,14 +90,21 @@ def tile_picked_mombondpagex_none_po_kernel(tc, x_words, x_scales, wa, wb, gt, g
             held[t] = tile
             nc.vector.tensor_scalar(held[t][:], page[t][:].indirect(n3_t[:]), 0.5, 0.0, ALU.mult, ALU.add)
 
-        def pick_tokens(name, offsets):
+        def pick_scales(name, offsets):
             listed = sb(f"{name}_listed", [P, S], U8)
             nc.vector.tensor_copy(listed[:], x_bytes[:].indirect(offsets[:]))
-            codes = sb(f"{name}_codes", [P, S], U32)
-            nc.vector.tensor_copy(codes[:].rearrange("p (t m) -> p m t", t=PACK), x_codes[:].bitcast(U32).indirect(offsets[:]))
+            return listed
+
+        def deal_scales(name, listed):
             scales = sb(f"{name}_scales", [P, S], U8)
-            nc.vector.tensor_copy(scales[:].rearrange("p (t m) -> p t m", t=PACK), listed[:].rearrange("p (m t) -> p t m", t=PACK))
-            return codes, scales
+            nc.vector.tensor_copy(scales[:].bitcast(I32).rearrange("p (t q h) -> p t q h", t=PACK, h=RUN // 4),
+                                  listed[:].bitcast(I32).rearrange("p (q t h) -> p t q h", t=PACK, h=RUN // 4))
+            return scales
+
+        def pick_codes(name, offsets):
+            codes = sb(f"{name}_codes", [P, S], U32)
+            nc.vector.tensor_copy(codes[:].rearrange("p (t q r) -> p q t r", t=PACK, r=RUN), x_codes[:].bitcast(U32).indirect(offsets[:]))
+            return codes
 
         def quantize(codes, scales, grouped):
             nc.vector.quantize_mx(out=codes.bitcast(FP8X4), scales=scales, in_=grouped.rearrange("p c t -> p (c t)"))
@@ -114,8 +130,12 @@ def tile_picked_mombondpagex_none_po_kernel(tc, x_words, x_scales, wa, wb, gt, g
             return acc
 
         fetch_held(0, sb("held0", [P, N], F32))
-        xa = pick_tokens("xa", offs_t)
-        xb = pick_tokens("xb", two_t)
+        xa_listed = pick_scales("xa", offs_t)
+        xb_listed = pick_scales("xb", two_t)
+        xa_scales = deal_scales("xa", xa_listed)
+        xb_scales = deal_scales("xb", xb_listed)
+        xa = (pick_codes("xa", offs_t), xa_scales)
+        xb = (pick_codes("xb", two_t), xb_scales)
         wa_q = quantize_weight("wa", wa_raw)
         a = []
         for t in range(PACK):
@@ -138,7 +158,7 @@ def tile_picked_mombondpagex_none_po_kernel(tc, x_words, x_scales, wa, wb, gt, g
             nc.scalar.activation(
                 z_grouped[:, :, t].rearrange("p (r m i) -> p m r i", r=PACK, i=2),
                 dt[t][:].rearrange("p (m i r) -> p m r i", r=PACK, i=2),
-                COPY, scale=gt_t[:, t:t + 1])
+                COPY, scale=gates[:, t:t + 1])
 
         fetch(pa, 0, n1_t)
         fetch(pb, 0, n2_t)
@@ -156,7 +176,7 @@ def tile_picked_mombondpagex_none_po_kernel(tc, x_words, x_scales, wa, wb, gt, g
         z2_planes = sb("z2_planes", [P, PACK, N], BF16)
         for t in range(PACK):
             acc = product("second", xb, wb_q, t)
-            nc.scalar.activation(z2_planes[:, t, :], acc[:], COPY, scale=gi_t[:, t:t + 1])
+            nc.scalar.activation(z2_planes[:, t, :], acc[:], COPY, scale=gates[:, PACK + t:PACK + t + 1])
         z2_grouped = sb("z2_grouped", [P, N, PACK], BF16)
         interleave(z2_grouped[:], z2_planes[:])
         z_grouped = sb("z_grouped", [P, H, PACK], BF16, "z2_planes")
@@ -207,12 +227,12 @@ def tile_picked_mombondpagex_none_po_kernel(tc, x_words, x_scales, wa, wb, gt, g
 
         out_scales = sb("out_scales", [P, U], U8)
         words = out_1[0].rearrange("p c r -> p (c r)").bitcast(I32)
-        for h in range(2):
-            out_codes = sb(f"out_codes{h}", [P, 2 * CHUNK], I32)
-            for i in range(2):
-                c = 2 * h + i
+        for first, last in ((0, 2), (2, 3), (3, 4)):
+            out_codes = sb(f"out_codes{first}", [P, (last - first) * CHUNK], I32)
+            for c in range(first, last):
+                i = c - first
                 quantize(out_codes[:, i * CHUNK:(i + 1) * CHUNK], out_scales[:, c * CHUNK:(c + 1) * CHUNK], out_grouped[c][:])
-            nc.sync.dma_start(words[:, 2 * h * CHUNK:2 * (h + 1) * CHUNK], out_codes[:])
+            nc.sync.dma_start(words[:, first * CHUNK:last * CHUNK], out_codes[:])
         for q in range(4):
             queue = nc.sync if q % 2 else nc.scalar
             queue.dma_start(out_2[0, 4 * q:4 * q + 4, :].bitcast(I32), out_scales[32 * q:32 * q + 4, :].bitcast(I32))

@@ -19,6 +19,7 @@ COPY = mybir.ActivationFunctionType.Copy
 P = 128
 PACK = 4
 RUN = 8
+GPSIMD_BYTES = 1280
 HALF = 256
 CHUNK = 256
 CHUNKS = U // CHUNK
@@ -50,31 +51,34 @@ def tile_picked_mombondpagex_none_po_kernel(tc, x_words, x_scales, wa, wb, gt, g
         def load_page(t):
             nc.sync.dma_start(page[t][:], mem_rows[t])
 
-        def load_weight_half(name, w, h):
-            raw = sb(f"{name}_raw{h}", [P, PACK, HALF], F32)
-            nc.sync.dma_start(raw[:], w.rearrange("(p j) c -> p j c", j=PACK)[:, :, h * HALF:(h + 1) * HALF])
-            return raw
+        def load_weight_half(raw, w, h):
+            nc.sync.dma_start(raw[h][:], w.rearrange("(p j) c -> p j c", j=PACK)[:, :, h * HALF:(h + 1) * HALF])
 
         x_bytes = sb("x_bytes", [P, T], U8)
-        nc.vector.memset(x_bytes[:].bitcast(I32), 0)
+        nc.gpsimd.memset(x_bytes[:, :GPSIMD_BYTES].bitcast(I32), 0)
+        nc.vector.memset(x_bytes[:, GPSIMD_BYTES:].bitcast(I32), 0)
         offs_t = load_list("offs_t", offs)
-        n3_t = load_list("n3_t", n3)
-        load_page(0)
+        two_t = load_list("two_t", two)
         for q in range(4):
             nc.sync.dma_start(x_bytes[32 * q:32 * q + 4, :].bitcast(I32), x_scales[0, 4 * q:4 * q + 4, :].bitcast(I32))
-        two_t = load_list("two_t", two)
-        n1_t = load_list("n1_t", n1)
+        n3_t = load_list("n3_t", n3)
         x_codes = sb("x_codes", [P, T], I32)
         nc.sync.dma_start(x_codes[:], x_words[0].rearrange("p c r -> p (c r)").bitcast(I32))
-        wa_raw = [load_weight_half("wa", wa, h) for h in range(2)]
-        load_page(1)
+        wa_raw = [sb(f"wa_raw{h}", [P, PACK, HALF], F32) for h in range(2)]
+        for h in range(2):
+            load_weight_half(wa_raw, wa, h)
+        load_page(0)
+        n1_t = load_list("n1_t", n1)
         n2_t = load_list("n2_t", n2)
-        wb_raw = [load_weight_half("wb", wb, h) for h in range(2)]
+        wb_raw = [sb("wb_raw0", [P, PACK, HALF], F32), placed("wb_raw1", [P, PACK, HALF], F32, 0)]
+        for h in range(2):
+            load_weight_half(wb_raw, wb, h)
         gate_rows = sb("gate_rows", [P, P], F32)
         nc.gpsimd.memset(gate_rows[:], 0.0)
         for i, gate in enumerate((gt, gi)):
             nc.sync.dma_start(gate_rows[PACK * i:PACK * (i + 1), :].rearrange("t (q r) -> t q r", r=RUN),
                                 gate.rearrange("(q t r) o -> t q (r o)", t=PACK, r=RUN))
+        load_page(1)
         load_page(2)
         load_page(3)
         identity = sb("identity", [P, P], F32)
@@ -129,7 +133,6 @@ def tile_picked_mombondpagex_none_po_kernel(tc, x_words, x_scales, wa, wb, gt, g
                                 rhs=right[0][:].bitcast(FP8X4), rhs_scale=right[1][:], start=True, stop=True)
             return acc
 
-        fetch_held(0, sb("held0", [P, N], F32))
         xa_listed = pick_scales("xa", offs_t)
         xb_listed = pick_scales("xb", two_t)
         xa_scales = deal_scales("xa", xa_listed)
@@ -142,7 +145,7 @@ def tile_picked_mombondpagex_none_po_kernel(tc, x_words, x_scales, wa, wb, gt, g
             acc = product("first", xa, wa_q, t)
             a.append(sb(f"a{t}", [P, H], F32))
             nc.scalar.copy(a[t][:], acc[:])
-        fetch_held(1, sb("held1", [P, N], F32, "wa_grouped1"))
+        fetch_held(0, sb("held0", [P, N], F32, "wa_raw1"))
 
         pa = [sb("pa0", [P, W], F32)]
         pb = [sb(f"pb{t}", [P, W], F32) for t in range(PACK)]
@@ -167,12 +170,12 @@ def tile_picked_mombondpagex_none_po_kernel(tc, x_words, x_scales, wa, wb, gt, g
         fetch(pb, 2, n2_t)
         put(0, n2_t, ALU.mult)
         fetch(pb, 3, n2_t)
-        wb_grouped = placed("wb_grouped", [P, N, PACK], BF16, 0)
+        wb_grouped = sb("wb_grouped", [P, N, PACK], BF16)
         for h in range(2):
             interleave(wb_grouped[:, h * HALF:(h + 1) * HALF, :], wb_raw[h][:])
         wb_q = (sb("wb_codes", [P, N], U32), sb("wb_scales", [P, N], U8))
         quantize(wb_q[0][:], wb_q[1][:], wb_grouped[:])
-        pa.extend(placed(f"pa{t}", [P, W], F32, 4 * W * t) for t in range(1, PACK))
+        pa.extend(placed(f"pa{t}", [P, W], F32, 4 * W * (t - 1)) for t in range(1, PACK))
         z2_planes = sb("z2_planes", [P, PACK, N], BF16)
         for t in range(PACK):
             acc = product("second", xb, wb_q, t)
@@ -195,10 +198,11 @@ def tile_picked_mombondpagex_none_po_kernel(tc, x_words, x_scales, wa, wb, gt, g
         quantize(z2_q[0][:], z2_q[1][:], z2_grouped[:])
         put(PACK - 1, n2_t, ALU.mult)
         round_z(PACK - 1)
-        fetch_held(2, placed("held2", [P, N], F32, 4 * W * (PACK - 1)))
+        fetch_held(1, sb("held1", [P, N], F32, "pb2"))
+        fetch_held(2, placed("held2", [P, N], F32, 0))
         z_q = (sb("z_codes", [P, H], U32), sb("z_scales", [P, H], U8))
         quantize(z_q[0][:], z_q[1][:], z_grouped[:])
-        fetch_held(3, sb("held3", [P, N], F32, "z2_planes"))
+        fetch_held(3, sb("held3", [P, N], F32, "dt3"))
 
         out_grouped = [sb(f"out_grouped{c}", [P, CHUNK, PACK], BF16) for c in range(CHUNKS)]
         nw = [sb(f"nw{t}", [P, N], F32) for t in range(PACK)]

@@ -58,16 +58,17 @@ def tile_picked_mombondpagex_none_po_kernel(tc, x_words, x_scales, wa, wb, gt, g
         nc.gpsimd.memset(x_bytes[:, :GPSIMD_BYTES].bitcast(I32), 0)
         nc.vector.memset(x_bytes[:, GPSIMD_BYTES:].bitcast(I32), 0)
         offs_t = load_list("offs_t", offs)
-        two_t = load_list("two_t", two)
+        n3_t = load_list("n3_t", n3)
+        load_page(0)
         for q in range(4):
             nc.sync.dma_start(x_bytes[32 * q:32 * q + 4, :].bitcast(I32), x_scales[0, 4 * q:4 * q + 4, :].bitcast(I32))
-        n3_t = load_list("n3_t", n3)
         x_codes = sb("x_codes", [P, T], I32)
         nc.sync.dma_start(x_codes[:], x_words[0].rearrange("p c r -> p (c r)").bitcast(I32))
+        two_t = load_list("two_t", two)
         wa_raw = [sb(f"wa_raw{h}", [P, PACK, HALF], F32) for h in range(2)]
         for h in range(2):
             load_weight_half(wa_raw, wa, h)
-        load_page(0)
+        load_page(1)
         n1_t = load_list("n1_t", n1)
         n2_t = load_list("n2_t", n2)
         wb_raw = [sb("wb_raw0", [P, PACK, HALF], F32), placed("wb_raw1", [P, PACK, HALF], F32, 0)]
@@ -78,7 +79,6 @@ def tile_picked_mombondpagex_none_po_kernel(tc, x_words, x_scales, wa, wb, gt, g
         for i, gate in enumerate((gt, gi)):
             nc.sync.dma_start(gate_rows[PACK * i:PACK * (i + 1), :].rearrange("t (q r) -> t q r", r=RUN),
                                 gate.rearrange("(q t r) o -> t q (r o)", t=PACK, r=RUN))
-        load_page(1)
         load_page(2)
         load_page(3)
         identity = sb("identity", [P, P], F32)
@@ -116,36 +116,36 @@ def tile_picked_mombondpagex_none_po_kernel(tc, x_words, x_scales, wa, wb, gt, g
         def interleave(grouped, planes):
             nc.scalar.copy(grouped.rearrange("p (c i) t -> p c t i", i=4), planes.rearrange("p t (c i) -> p c t i", i=4))
 
-        def quantize_weight(name, raw):
-            codes = sb(f"{name}_codes", [P, 2 * HALF], U32)
-            scales = sb(f"{name}_scales", [P, 2 * HALF], U8)
-            for h in range(2):
-                grouped = sb(f"{name}_grouped{h}", [P, HALF, PACK], BF16)
-                interleave(grouped[:], raw[h][:])
-                cols = slice(h * HALF, (h + 1) * HALF)
-                quantize(codes[:, cols], scales[:, cols], grouped[:])
-            return codes, scales
+        def multiply(acc, left, right, t, cols):
+            rows = slice(t * P, (t + 1) * P)
+            nc.tensor.matmul_mx(out=acc[:, cols], lhsT=left[0][:, rows].bitcast(FP8X4), lhsT_scale=left[1][:, rows],
+                                rhs=right[0][:, cols].bitcast(FP8X4), rhs_scale=right[1][:, cols], start=True, stop=True)
 
         def product(tag, left, right, t):
-            acc = psum.tile([P, 512], F32, name=f"{tag}_acc", tag=tag)
-            cols = slice(t * P, (t + 1) * P)
-            nc.tensor.matmul_mx(out=acc[:], lhsT=left[0][:, cols].bitcast(FP8X4), lhsT_scale=left[1][:, cols],
-                                rhs=right[0][:].bitcast(FP8X4), rhs_scale=right[1][:], start=True, stop=True)
+            acc = psum.tile([P, N], F32, name=f"{tag}_acc", tag=tag)
+            multiply(acc, left, right, t, slice(0, N))
             return acc
 
+        fetch_held(0, sb("held0", [P, N], F32))
         xa_listed = pick_scales("xa", offs_t)
         xb_listed = pick_scales("xb", two_t)
         xa_scales = deal_scales("xa", xa_listed)
         xb_scales = deal_scales("xb", xb_listed)
         xa = (pick_codes("xa", offs_t), xa_scales)
         xb = (pick_codes("xb", two_t), xb_scales)
-        wa_q = quantize_weight("wa", wa_raw)
-        a = []
+        wa_q = (sb("wa_codes", [P, H], U32), sb("wa_scales", [P, H], U8))
+        a_acc = [psum.tile([P, H], F32, name="a_acc", tag="first") for t in range(PACK)]
+        for h in range(2):
+            cols = slice(h * HALF, (h + 1) * HALF)
+            wa_grouped = sb(f"wa_grouped{h}", [P, HALF, PACK], BF16)
+            interleave(wa_grouped[:], wa_raw[h][:])
+            quantize(wa_q[0][:, cols], wa_q[1][:, cols], wa_grouped[:])
+            for t in range(PACK):
+                multiply(a_acc[t], xa, wa_q, t, cols)
+        a = [sb(f"a{t}", [P, H], F32) for t in range(PACK)]
         for t in range(PACK):
-            acc = product("first", xa, wa_q, t)
-            a.append(sb(f"a{t}", [P, H], F32))
-            nc.scalar.copy(a[t][:], acc[:])
-        fetch_held(0, sb("held0", [P, N], F32, "wa_raw1"))
+            nc.scalar.copy(a[t][:], a_acc[t][:])
+        fetch_held(1, sb("held1", [P, N], F32, "wa_raw1"))
 
         pa = [sb("pa0", [P, W], F32)]
         pb = [sb(f"pb{t}", [P, W], F32) for t in range(PACK)]
@@ -157,10 +157,10 @@ def tile_picked_mombondpagex_none_po_kernel(tc, x_words, x_scales, wa, wb, gt, g
         def put(t, offsets, op):
             nc.vector.tensor_tensor(dt[t][:].indirect(offsets[:]), pa[t][:], pb[t][:], op)
 
-        def round_z(t):
+        def round_z(t, tiles=slice(0, PACK)):
             nc.scalar.activation(
-                z_grouped[:, :, t].rearrange("p (r m i) -> p m r i", r=PACK, i=2),
-                dt[t][:].rearrange("p (m i r) -> p m r i", r=PACK, i=2),
+                z_grouped[:, :, t].rearrange("p (r m i) -> p m r i", r=PACK, i=2)[:, :, tiles, :],
+                dt[t][:].rearrange("p (m i r) -> p m r i", r=PACK, i=2)[:, :, tiles, :],
                 COPY, scale=gates[:, t:t + 1])
 
         fetch(pa, 0, n1_t)
@@ -197,11 +197,13 @@ def tile_picked_mombondpagex_none_po_kernel(tc, x_words, x_scales, wa, wb, gt, g
         z2_q = (sb("z2_codes", [P, N], U32), sb("z2_scales", [P, N], U8))
         quantize(z2_q[0][:], z2_q[1][:], z2_grouped[:])
         put(PACK - 1, n2_t, ALU.mult)
-        round_z(PACK - 1)
-        fetch_held(1, sb("held1", [P, N], F32, "pb2"))
+        for h in range(2):
+            round_z(PACK - 1, slice(2 * h, 2 * h + 2))
         fetch_held(2, placed("held2", [P, N], F32, 0))
         z_q = (sb("z_codes", [P, H], U32), sb("z_scales", [P, H], U8))
-        quantize(z_q[0][:], z_q[1][:], z_grouped[:])
+        for h in range(2):
+            cols = slice(h * HALF, (h + 1) * HALF)
+            quantize(z_q[0][:, cols], z_q[1][:, cols], z_grouped[:, cols, :])
         fetch_held(3, sb("held3", [P, N], F32, "dt3"))
 
         out_grouped = [sb(f"out_grouped{c}", [P, CHUNK, PACK], BF16) for c in range(CHUNKS)]

from contextlib import ExitStack

import concourse.mybir as mybir
from concourse.masks import make_identity

K, T, S, N, H, W, U = 512, 2048, 512, 512, 512, 256, 1024
FLOPS = 2 * K * S * H + 2 * K * S * N + 2 * S * H * N

F32 = mybir.dt.float32
BF16 = mybir.dt.bfloat16
I32 = mybir.dt.int32
U32 = mybir.dt.uint32
U16 = mybir.dt.uint16
U8 = mybir.dt.uint8
FP8X4 = mybir.dt.float8_e4m3fn_x4
ALU = mybir.AluOpType
COPY = mybir.ActivationFunctionType.Copy

P = 128
PACK = 4
RUN = 8
GPSIMD_BYTES = 1280
HALF = 256
CHUNK = 256
CHUNKS = U // CHUNK
VECTOR_CHUNKS = 2


def tile_picked_mombondpagex_none_po_kernel(tc, x_words, x_scales, wa, wb, gt, gi, mem, offs, two, n1, n2, n3, out_0, out_1, out_2):
    nc = tc.nc
    with ExitStack() as ctx:
        keep = ctx.enter_context(tc.tile_pool(name="keep", bufs=1))
        shared = ctx.enter_context(tc.tile_pool(name="shared", bufs=1))
        psum = ctx.enter_context(tc.psum_pool(name="psum", bufs=4))

        def sb(name, shape, dtype, tag=None):
            return keep.tile(shape, dtype, name=name, tag=tag or name, align_bytes=64)

        def placed(name, shape, dtype, offset):
            return shared.tile(shape, dtype, name=name, align_bytes=64, offset=offset)

        def load_list(name, src):
            tile = sb(name, list(src.shape), U16)
            nc.sync.dma_start(tile[:], src)
            return tile

        mem_rows = mem.rearrange("(p t) u -> t p u", t=PACK)
        out_rows = out_0.rearrange("(p t) u -> t p u", t=PACK)
        page = [sb(f"page{t}", [P, U], F32) for t in range(PACK)]

        def load_page(t):
            nc.sync.dma_start(page[t][:], mem_rows[t])

        def load_weight_half(raw, w, h):
            nc.sync.dma_start(raw[h][:], w.rearrange("(p j) c -> p j c", j=PACK)[:, :, h * HALF:(h + 1) * HALF])

        x_bytes = sb("x_bytes", [P, T], U8)
        nc.gpsimd.memset(x_bytes[:, :GPSIMD_BYTES].bitcast(I32), 0)
        nc.vector.memset(x_bytes[:, GPSIMD_BYTES:].bitcast(I32), 0)
        offs_t = load_list("offs_t", offs)
        n3_t = load_list("n3_t", n3)
        load_page(0)
        for q in range(4):
            nc.sync.dma_start(x_bytes[32 * q:32 * q + 4, :].bitcast(I32), x_scales[0, 4 * q:4 * q + 4, :].bitcast(I32))
        x_codes = sb("x_codes", [P, T], I32)
        nc.sync.dma_start(x_codes[:], x_words[0].rearrange("p c r -> p (c r)").bitcast(I32))
        two_t = load_list("two_t", two)
        wa_raw = [sb(f"wa_raw{h}", [P, PACK, HALF], F32) for h in range(2)]
        for h in range(2):
            load_weight_half(wa_raw, wa, h)
        load_page(1)
        n1_t = load_list("n1_t", n1)
        n2_t = load_list("n2_t", n2)
        wb_raw = [sb("wb_raw0", [P, PACK, HALF], F32), placed("wb_raw1", [P, PACK, HALF], F32, 0)]
        for h in range(2):
            load_weight_half(wb_raw, wb, h)
        gate_rows = sb("gate_rows", [P, P], F32)
        nc.gpsimd.memset(gate_rows[:], 0.0)
        for i, gate in enumerate((gt, gi)):
            nc.sync.dma_start(gate_rows[PACK * i:PACK * (i + 1), :].rearrange("t (q r) -> t q r", r=RUN),
                                gate.rearrange("(q t r) o -> t q (r o)", t=PACK, r=RUN))
        load_page(2)
        load_page(3)
        identity = sb("identity", [P, P], F32)
        make_identity(nc, identity[:])
        gate_acc = psum.tile([P, P], F32, name="gate_acc", tag="second")
        nc.tensor.transpose(gate_acc[:], gate_rows[:], identity[:])
        gates = sb("gates", [P, 2 * PACK], F32)
        nc.scalar.copy(gates[:], gate_acc[:, :2 * PACK])

        held = [None] * PACK

        def fetch_held(t, tile):
            held[t] = tile
            nc.vector.tensor_scalar(held[t][:], page[t][:].indirect(n3_t[:]), 0.5, 0.0, ALU.mult, ALU.add)

        def pick_scales(name, offsets):
            listed = sb(f"{name}_listed", [P, S], U8)
            nc.vector.tensor_copy(listed[:], x_bytes[:].indirect(offsets[:]))
            return listed

        def deal_scales(name, listed):
            scales = sb(f"{name}_scales", [P, S], U8)
            nc.vector.tensor_copy(scales[:].bitcast(I32).rearrange("p (t q h) -> p t q h", t=PACK, h=RUN // 4),
                                  listed[:].bitcast(I32).rearrange("p (q t h) -> p t q h", t=PACK, h=RUN // 4))
            return scales

        def pick_codes(name, offsets):
            codes = sb(f"{name}_codes", [P, S], U32)
            nc.vector.tensor_copy(codes[:].rearrange("p (t q r) -> p q t r", t=PACK, r=RUN), x_codes[:].bitcast(U32).indirect(offsets[:]))
            return codes

        def quantize(codes, scales, grouped):
            nc.vector.quantize_mx(out=codes.bitcast(FP8X4), scales=scales, in_=grouped.rearrange("p c t -> p (c t)"))

        def interleave(grouped, planes):
            nc.scalar.copy(grouped.rearrange("p (c i) t -> p c t i", i=4), planes.rearrange("p t (c i) -> p c t i", i=4))

        def multiply(acc, left, right, t, cols):
            rows = slice(t * P, (t + 1) * P)
            nc.tensor.matmul_mx(out=acc[:, cols], lhsT=left[0][:, rows].bitcast(FP8X4), lhsT_scale=left[1][:, rows],
                                rhs=right[0][:, cols].bitcast(FP8X4), rhs_scale=right[1][:, cols], start=True, stop=True)

        def product(tag, left, right, t):
            acc = psum.tile([P, N], F32, name=f"{tag}_acc", tag=tag)
            multiply(acc, left, right, t, slice(0, N))
            return acc

        fetch_held(0, sb("held0", [P, N], F32))
        xa_listed = pick_scales("xa", offs_t)
        xb_listed = pick_scales("xb", two_t)
        xa_scales = deal_scales("xa", xa_listed)
        xb_scales = deal_scales("xb", xb_listed)
        xa = (pick_codes("xa", offs_t), xa_scales)
        xb = (pick_codes("xb", two_t), xb_scales)
        wa_q = (sb("wa_codes", [P, H], U32), sb("wa_scales", [P, H], U8))
        a_acc = [psum.tile([P, H], F32, name="a_acc", tag="first") for t in range(PACK)]
        for h in range(2):
            cols = slice(h * HALF, (h + 1) * HALF)
            wa_grouped = sb(f"wa_grouped{h}", [P, HALF, PACK], BF16)
            interleave(wa_grouped[:], wa_raw[h][:])
            quantize(wa_q[0][:, cols], wa_q[1][:, cols], wa_grouped[:])
            for t in range(PACK):
                multiply(a_acc[t], xa, wa_q, t, cols)
        a = [sb(f"a{t}", [P, H], F32) for t in range(PACK)]
        for t in range(PACK):
            nc.scalar.copy(a[t][:], a_acc[t][:])
        fetch_held(1, sb("held1", [P, N], F32, "wa_raw1"))

        pa = [sb("pa0", [P, W], F32)]
        pb = [sb(f"pb{t}", [P, W], F32) for t in range(PACK)]
        dt = [sb(f"dt{t}", [P, H], F32) for t in range(PACK)]

        def fetch(dst, t, offsets):
            nc.vector.tensor_copy(dst[t][:], a[t][:].indirect(offsets[:]))

        def put(t, offsets, op):
            nc.vector.tensor_tensor(dt[t][:].indirect(offsets[:]), pa[t][:], pb[t][:], op)

        def round_z(t, tiles=slice(0, PACK)):
            nc.scalar.activation(
                z_grouped[:, :, t].rearrange("p (r m i) -> p m r i", r=PACK, i=2)[:, :, tiles, :],
                dt[t][:].rearrange("p (m i r) -> p m r i", r=PACK, i=2)[:, :, tiles, :],
                COPY, scale=gates[:, t:t + 1])

        fetch(pa, 0, n1_t)
        fetch(pb, 0, n2_t)
        fetch(pb, 1, n2_t)
        put(0, n1_t, ALU.add)
        fetch(pb, 2, n2_t)
        put(0, n2_t, ALU.mult)
        fetch(pb, 3, n2_t)
        wb_grouped = sb("wb_grouped", [P, N, PACK], BF16)
        for h in range(2):
            interleave(wb_grouped[:, h * HALF:(h + 1) * HALF, :], wb_raw[h][:])
        wb_q = (sb("wb_codes", [P, N], U32), sb("wb_scales", [P, N], U8))
        quantize(wb_q[0][:], wb_q[1][:], wb_grouped[:])
        pa.extend(placed(f"pa{t}", [P, W], F32, 4 * W * (t - 1)) for t in range(1, PACK))
        z2_planes = sb("z2_planes", [P, PACK, N], BF16)
        for t in range(PACK):
            acc = product("second", xb, wb_q, t)
            nc.scalar.activation(z2_planes[:, t, :], acc[:], COPY, scale=gates[:, PACK + t:PACK + t + 1])
        z2_grouped = sb("z2_grouped", [P, N, PACK], BF16)
        interleave(z2_grouped[:], z2_planes[:])
        z_grouped = sb("z_grouped", [P, H, PACK], BF16, "z2_planes")
        round_z(0)
        fetch(pa, 1, n1_t)
        fetch(pa, 2, n1_t)
        put(1, n1_t, ALU.add)
        fetch(pa, 3, n1_t)
        put(1, n2_t, ALU.mult)
        round_z(1)
        put(2, n1_t, ALU.add)
        put(3, n1_t, ALU.add)
        put(2, n2_t, ALU.mult)
        round_z(2)
        z2_q = (sb("z2_codes", [P, N], U32), sb("z2_scales", [P, N], U8))
        quantize(z2_q[0][:], z2_q[1][:], z2_grouped[:])
        put(PACK - 1, n2_t, ALU.mult)
        for h in range(2):
            round_z(PACK - 1, slice(2 * h, 2 * h + 2))
        fetch_held(2, placed("held2", [P, N], F32, 0))
        z_q = (sb("z_codes", [P, H], U32), sb("z_scales", [P, H], U8))
        for h in range(2):
            cols = slice(h * HALF, (h + 1) * HALF)
            quantize(z_q[0][:, cols], z_q[1][:, cols], z_grouped[:, cols, :])
        fetch_held(3, sb("held3", [P, N], F32, "dt3"))

        out_grouped = [sb(f"out_grouped{c}", [P, CHUNK, PACK], BF16) for c in range(CHUNKS)]
        nw = [sb(f"nw{t}", [P, N], F32) for t in range(PACK)]

        def larger(t):
            acc = product("first", z_q, z2_q, t)
            nc.vector.scalar_tensor_tensor(nw[t][:], acc[:], 0.0625, held[t][:], ALU.mult, ALU.max)

        def write(t):
            nc.vector.tensor_copy(page[t][:].indirect(n3_t[:]), nw[t][:])
            nc.sync.dma_start(out_rows[t], page[t][:])
            for c in range(CHUNKS):
                src = page[t][:, c * CHUNK:(c + 1) * CHUNK]
                if t == PACK - 1 and c < VECTOR_CHUNKS:
                    nc.vector.tensor_copy(out_grouped[c][:, :, t], src)
                elif t == PACK - 2 and c < VECTOR_CHUNKS:
                    nc.scalar.copy(out_grouped[c][:, :, t:], src.unsqueeze(2).to_broadcast([P, CHUNK, 2]))
                else:
                    nc.scalar.copy(out_grouped[c][:, :, t], src)

        larger(0)
        for t in range(PACK):
            if t + 1 < PACK:
                larger(t + 1)
            write(t)

        out_scales = sb("out_scales", [P, U], U8)
        words = out_1[0].rearrange("p c r -> p (c r)").bitcast(I32)
        for first, last in ((0, 2), (2, 3), (3, 4)):
            out_codes = sb(f"out_codes{first}", [P, (last - first) * CHUNK], I32)
            for c in range(first, last):
                i = c - first
                quantize(out_codes[:, i * CHUNK:(i + 1) * CHUNK], out_scales[:, c * CHUNK:(c + 1) * CHUNK], out_grouped[c][:])
            nc.sync.dma_start(words[:, first * CHUNK:last * CHUNK], out_codes[:])
        for q in range(4):
            queue = nc.sync if q % 2 else nc.scalar
            queue.dma_start(out_2[0, 4 * q:4 * q + 4, :].bitcast(I32), out_scales[32 * q:32 * q + 4, :].bitcast(I32))
